import numpy as np
import ml_dtypes


def mxq(x, axis, fmt="e4m3"):
    dtype, down = {"e4m3": (ml_dtypes.float8_e4m3fn, 7), "e5m2": (ml_dtypes.float8_e5m2, 14)}[fmt]
    v = np.moveaxis(np.asarray(x, np.float32).astype(ml_dtypes.bfloat16).astype(np.float64), axis, -1)
    blocks = v.reshape(v.shape[:-1] + (-1, 32))
    amax = np.abs(blocks).max(-1, keepdims=True)
    byte = np.maximum(np.where(amax > 0, np.frexp(amax)[1] - 1 + 127, 0) - down, 1)
    scale = np.exp2(byte - 127.0)
    codes = (blocks / scale).astype(np.float32).astype(dtype).astype(np.float64)
    return np.moveaxis((codes * scale).reshape(v.shape), -1, axis)


WIDE = False


def mx_kscale(k):
    if not WIDE:
        return np.ones(k)
    levels = np.array([10, -10, 5, -5, 0])
    if k % 512:
        return np.exp2(np.random.permutation(np.resize(levels, k // 32))).repeat(32)
    a = np.empty((k // 512, 16))
    for p in range(k // 512):
        a[p, :8] = np.random.permutation(np.resize(levels, 8))
        for g in range(8):
            far = levels[np.abs(levels - a[p, g]) >= 10]
            a[p, g + 8] = far[np.random.randint(len(far))]
    return np.exp2(a.ravel()).repeat(32)


def f64(x):
    return np.asarray(x).astype(np.float64)


def striped(idx):
    return np.tile(idx.reshape(-1, 16).T, (8, 1)).astype(np.uint16)


def unstriped(offs):
    return offs[:16].T.reshape(-1).astype(np.int64)


def striped8(idx):
    return np.concatenate([x.reshape(-1, 16).T for x in idx]).astype(np.uint16)


def runs(offs, k):
    lists = np.stack([offs[16 * r : 16 * r + 16].T.reshape(-1) for r in range(8)]).astype(np.int64)
    return lists[np.arange(k) % 512 // 64]


def pack_weight(w):
    k, n = w.shape
    w = f64(np.asarray(w, np.float32).astype(ml_dtypes.bfloat16)).reshape(k // 32, 32, n)
    amax = np.abs(w).max(1)
    byte = np.clip(np.where(amax > 0, np.frexp(amax)[1] - 1 + 127 - 7, 1), 1, 254)
    scaled = (w * np.exp2(127.0 - byte)[:, None, :]).reshape(k, n).astype(np.float32)
    words = np.ascontiguousarray(scaled.reshape(k // 512, 128, 4, n).transpose(0, 1, 3, 2)).astype(ml_dtypes.float8_e4m3fn).view(np.uint8)
    return words, np.ascontiguousarray(byte.astype(np.uint8).reshape(k // 512, 16, n))


def unpack_weight(words, scales):
    g, p, n, _ = words.shape
    vals = np.ascontiguousarray(words).view(ml_dtypes.float8_e4m3fn).astype(np.float64) * np.repeat(np.exp2(scales.astype(np.float64) - 127.0), 8, axis=1)[..., None]
    return vals.transpose(0, 1, 3, 2).reshape(g * 512, n)

def planes(y):
    n, m = y.shape
    v = y.astype(np.float32).astype(ml_dtypes.bfloat16).astype(np.float64).reshape(n // 32, 32, m)
    top = np.abs(v).max(1)
    byte = np.clip(np.where(top > 0, np.frexp(top)[1] - 1 + 127 - 7, 1), 1, 254)
    codes = (v * np.exp2(127.0 - byte)[:, None, :]).reshape(n, m).astype(np.float32).astype(ml_dtypes.float8_e4m3fn).view(np.uint8)
    words = codes.reshape(n // 512, 128, 4, m).transpose(0, 1, 3, 2)
    return np.ascontiguousarray(words), np.ascontiguousarray(byte.astype(np.uint8).reshape(n // 512, 16, m))


K, T, S, H, G, W = 512, 1024, 512, 512, 2048, 256


def setup_inputs():
    n = np.random.standard_normal
    s = mx_kscale(K)[:, None]
    packed_xT = pack_weight(n((K, T)) * s)
    packed_w1 = pack_weight(n((K, H)) / np.sqrt(K) / s)
    packed_w2 = pack_weight(n((K, H)) / np.sqrt(K) / s)
    packed_dT = pack_weight(n((K, G)) / s)
    perm = np.stack([np.random.permutation(S) for _ in range(8)])
    return {
        "x_words": packed_xT[0],
        "x_scales": packed_xT[1],
        "w1_words": packed_w1[0],
        "w1_scales": packed_w1[1],
        "w2_words": packed_w2[0],
        "w2_scales": packed_w2[1],
        "gs": (np.random.uniform(0.5, 1.5, (K, 1)) * s).astype(np.float32),
        "d_words": packed_dT[0],
        "d_scales": packed_dT[1],
        "offs": striped(np.random.permutation(T)[:S]),
        "two": striped(np.random.permutation(T)[:S]),
        "n1": striped8(np.stack([np.random.permutation(S) for _ in range(8)])),
        "n2": striped8(np.stack([np.random.permutation(S) for _ in range(8)])),
        "k1": striped8(np.random.randint(0, G, (8, H))),
        "n3": striped8(perm[:, :W]),
        "n4": striped8(perm[:, W:]),
    }


def reference(x_words, x_scales, w1_words, w1_scales, w2_words, w2_scales, gs, d_words, d_scales, offs, two, n1, n2, k1, n3, n4):
    d_k1 = unpack_weight(d_words, d_scales)[np.arange(K)[:, None], runs(k1, K)]
    xq = unpack_weight(x_words, x_scales)[:, unstriped(offs)]
    y = unpack_weight(w1_words, w1_scales).T @ xq
    x_two = unpack_weight(x_words, x_scales)[:, unstriped(two)]
    d = unpack_weight(w2_words, w2_scales).T @ x_two
    z = f64(gs) * ((y - (y[np.arange(H)[:, None], runs(n1, H)])) / (np.abs(d) + np.abs(d[np.arange(H)[:, None], runs(n2, H)]) + 0.5))
    h = 0.0625 * ((d_k1.T @ mxq(z, 0, "e4m3")))
    pa = h[np.arange(H)[:, None], runs(n3, H)]
    pb = h[np.arange(H)[:, None], runs(n4, H)]
    rb = np.maximum(pa, pb)
    ra = pa / (np.abs(pb) + 0.5)
    ds = np.zeros((H, S))
    ds[np.arange(H)[:, None], runs(n3, H)] = ra
    out = ds.copy()
    out[np.arange(H)[:, None], runs(n4, H)] = rb
    return (out,) + planes(out)

@@ -1,0 +1,240 @@
+from contextlib import ExitStack
+
+import concourse.mybir as mybir
+
+K, T, S, H, G, W = 512, 1024, 512, 512, 2048, 256
+FLOPS = 3 * 2 * K * H * S
+
+F32 = mybir.dt.float32
+BF16 = mybir.dt.bfloat16
+I32 = mybir.dt.int32
+U32 = mybir.dt.uint32
+U16 = mybir.dt.uint16
+U8 = mybir.dt.uint8
+FP8X4 = mybir.dt.float8_e4m3fn_x4
+ACT = mybir.ActivationFunctionType
+ALU = mybir.AluOpType
+
+P = 128
+PACK = 4
+HALF = S // 2
+
+
+def tile_picked_twqnormbratio_none_po_kernel(
+    tc, x_words, x_scales, w1_words, w1_scales, w2_words, w2_scales, gs, d_words, d_scales,
+    offs, two, n1, n2, k1, n3, n4, out_0, out_1, out_2,
+):
+    nc = tc.nc
+    with ExitStack() as ctx:
+        keep = ctx.enter_context(tc.tile_pool(name="keep", bufs=1))
+        psum = ctx.enter_context(tc.psum_pool(name="psum", bufs=1))
+
+        def sb(name, shape, dtype):
+            return keep.tile(shape, dtype, name=name, align_bytes=64)
+
+        def load_list(name, src):
+            t = keep.tile(list(src.shape), U16, name=name)
+            nc.sync.dma_start(t[:], src)
+            return t
+
+        def load_words(name, src):
+            t = sb(name, [P, src.shape[2]], U32)
+            nc.sync.dma_start(t[:].bitcast(I32), src[0].rearrange("p n r -> p (n r)").bitcast(I32))
+            return t
+
+        def load_scale_rows(queue, t, first, src):
+            for q in range(4):
+                queue.dma_start(
+                    t[32 * q + first : 32 * q + first + 4, :].bitcast(I32),
+                    src[0, 4 * q : 4 * q + 4, :].bitcast(I32),
+                )
+
+        def deal(dst, src):
+            nc.vector.tensor_copy(dst[:].rearrange("p (t m) -> p m t", t=PACK), src[:].rearrange("p (m t) -> p m t", t=PACK))
+
+        x_sc = sb("x_sc", [P, T], U8)
+        w_sc = sb("w_sc", [P, H], U8)
+        d_sc = sb("d_sc", [P, G], U8)
+        dk_plane = sb("dk_plane", [P, H], U8)
+        half = sb("half", [P, 1], F32)
+        warm = sb("warm", [P, 1], F32)
+        for t in (x_sc, w_sc, d_sc, dk_plane):
+            nc.vector.memset(t[:].bitcast(I32), 0)
+        nc.vector.memset(half[:], 0.5)
+
+        x_wd = load_words("x_wd", x_words)
+        two_l = load_list("two_l", two)
+        load_scale_rows(nc.scalar, x_sc, 0, x_scales)
+        w2_wd = load_words("w2_wd", w2_words)
+        load_scale_rows(nc.scalar, w_sc, 0, w2_scales)
+        load_scale_rows(nc.sync, w_sc, 4, w1_scales)
+        nc.scalar.activation(warm[:], half[:], ACT.Abs_reciprocal_sqrt)
+        offs_l = load_list("offs_l", offs)
+        w1_wd = load_words("w1_wd", w1_words)
+        nc.sync.dma_start(d_sc[0:P:8, :].bitcast(I32), d_scales[0].bitcast(I32))
+        k1_l = load_list("k1_l", k1)
+        d_wd = load_words("d_wd", d_words)
+        n2_l = load_list("n2_l", n2)
+        gain = sb("gain", [P, PACK], F32)
+        nc.sync.dma_start(gain[:], gs.rearrange("(p t) o -> p (t o)", t=PACK))
+        n1_l = load_list("n1_l", n1)
+        n3_l = load_list("n3_l", n3)
+        n4_l = load_list("n4_l", n4)
+
+        neg_gain = sb("neg_gain", [P, PACK], F32)
+        nc.scalar.activation(neg_gain[:], gain[:], ACT.Copy, scale=-1.0)
+
+        def pick(name, table, lst, dtype):
+            t = sb(name, [P, S], dtype)
+            nc.vector.tensor_copy(t[:], table[:].indirect(lst[:]))
+            return t
+
+        x2_wd = pick("x2_wd", x_wd, two_l, U32)
+        x2_sc = pick("x2_sc", x_sc, two_l, U8)
+        w2_dealt = sb("w2_dealt", [P, H], I32)
+        deal(w2_dealt, w2_wd[:].bitcast(I32))
+        w_sc_dealt = sb("w_sc_dealt", [P, H], U8)
+        deal(w_sc_dealt, w_sc)
+        x1_wd = pick("x1_wd", x_wd, offs_l, U32)
+        x1_sc = pick("x1_sc", x_sc, offs_l, U8)
+        w1_dealt = sb("w1_dealt", [P, H], I32)
+        deal(w1_dealt, w1_wd[:].bitcast(I32))
+
+        dk_sc = pick("dk_sc", d_sc, k1_l, U8)
+        dk_sc_dealt = sb("dk_sc_dealt", [P, H], U8)
+        deal(dk_sc_dealt, dk_sc)
+        for q in range(4):
+            nc.sync.dma_start(
+                dk_plane[32 * q : 32 * q + 4, :].bitcast(I32),
+                dk_sc_dealt[32 * q : 32 * q + 32 : 8, :].bitcast(I32),
+            )
+        dk_wd = pick("dk_wd", d_wd, k1_l, U32)
+        dk_dealt = sb("dk_dealt", [P, H], I32)
+        deal(dk_dealt, dk_wd[:].bitcast(I32))
+
+        def rows(t):
+            return slice(P * t, P * (t + 1))
+
+        d_abs, d_abs2, y_win, y_plain = [], [], [], []
+        for t in range(PACK):
+            acc = psum.tile([P, S], F32, name=f"d_acc{t}", tag=f"bank{t}")
+            nc.tensor.matmul_mx(acc[:], lhsT=w2_dealt[:, rows(t)].bitcast(FP8X4), lhsT_scale=w_sc_dealt[:, rows(t)],
+                                rhs=x2_wd[:].bitcast(FP8X4), rhs_scale=x2_sc[:], start=True, stop=True)
+            d_abs.append(sb(f"d_abs{t}", [P, S], F32))
+            d_abs2.append(sb(f"d_own{t}", [P, S], F32))
+            nc.scalar.activation(d_abs[t][:], acc[:], ACT.Abs)
+            nc.scalar.activation(d_abs2[t][:], acc[:], ACT.Abs)
+        for t in range(PACK):
+            acc = psum.tile([P, S], F32, name=f"y_acc{t}", tag=f"bank{4 + t}")
+            nc.tensor.matmul_mx(acc[:], lhsT=w1_dealt[:, rows(t)].bitcast(FP8X4), lhsT_scale=w_sc_dealt[4:P, rows(t)],
+                                rhs=x1_wd[:].bitcast(FP8X4), rhs_scale=x1_sc[:], start=True, stop=True)
+            y_win.append(sb(f"y_win{t}", [P, S], F32))
+            y_plain.append(sb(f"y_own{t}", [P, S], F32))
+            nc.scalar.activation(y_win[t][:], acc[:], ACT.Copy, scale=neg_gain[:, t : t + 1])
+            nc.scalar.activation(y_plain[t][:], acc[:], ACT.Copy, scale=neg_gain[:, t : t + 1])
+
+        den = sb("den", [P, PACK, S], F32)
+        root = sb("root", [P, PACK, S], F32)
+        inv = sb("inv", [P, PACK, S], F32)
+        num = sb("num", [P, PACK, S], F32)
+        z = sb("z", [P, S, PACK], BF16)
+        z_wd = sb("z_wd", [P, S], U32)
+        z_sc = sb("z_sc", [P, S], U8)
+        h = [sb(f"h{t}", [P, S], F32) for t in range(PACK)]
+
+        halves = [slice(HALF * u, HALF * (u + 1)) for u in range(2)]
+        quarters = [slice(HALF, HALF + HALF // 2), slice(HALF + HALF // 2, S)]
+
+        def entries(cols):
+            return slice(cols.start // 16, cols.stop // 16)
+
+        def numerator(t, cols):
+            nc.vector.tensor_tensor(num[:, t, cols], y_win[t][:].indirect(n1_l[:, entries(cols)]), y_plain[t][:, cols], ALU.subtract)
+
+        def ratio(cols):
+            nc.vector.tensor_tensor(
+                z[:, cols, :].rearrange("p (c i) t -> p c t i", i=4),
+                num[:, :, cols].rearrange("p t (c i) -> p c t i", i=4),
+                inv[:, :, cols].rearrange("p t (c i) -> p c t i", i=4),
+                ALU.mult,
+            )
+
+        def quantize_z(cols):
+            nc.vector.quantize_mx(z_wd[:, cols].bitcast(FP8X4), z_sc[:, cols], z[:, cols, :].rearrange("p c t -> p (c t)"))
+
+        def coded(acc, t, cols):
+            nc.tensor.matmul_mx(acc[:, cols], lhsT=dk_dealt[:, rows(t)].bitcast(FP8X4), lhsT_scale=dk_plane[:, rows(t)],
+                                rhs=z_wd[:, cols].bitcast(FP8X4), rhs_scale=z_sc[:, cols], start=True, stop=True)
+
+        for cols in halves:
+            for t in range(PACK):
+                nc.vector.tensor_tensor(den[:, t, cols], d_abs[t][:].indirect(n2_l[:, entries(cols)]), d_abs2[t][:, cols], ALU.add)
+                nc.scalar.activation(root[:, t, cols], den[:, t, cols], ACT.Abs_reciprocal_sqrt, bias=half[:])
+                nc.scalar.activation(inv[:, t, cols], root[:, t, cols], ACT.Square)
+        for t in range(PACK):
+            numerator(t, halves[0])
+        for t in range(PACK - 1):
+            numerator(t, halves[1])
+        ratio(halves[0])
+        numerator(PACK - 1, halves[1])
+        quantize_z(halves[0])
+        for t in range(PACK):
+            acc = psum.tile([P, S], F32, name=f"h_lo{t}", tag=f"bank{t}")
+            coded(acc, t, halves[0])
+            nc.scalar.activation(h[t][:, halves[0]], acc[:, halves[0]], ACT.Copy, scale=0.0625)
+        for cols in quarters:
+            ratio(cols)
+        for cols in quarters:
+            quantize_z(cols)
+        h_hi = [psum.tile([P, S], F32, name=f"h_hi{t}", tag=f"bank{4 + t}") for t in range(PACK)]
+        for cols in quarters:
+            for t in range(PACK):
+                coded(h_hi[t], t, cols)
+        for t in range(PACK):
+            nc.scalar.activation(h[t][:, halves[1]], h_hi[t][:, halves[1]], ACT.Copy, scale=0.0625)
+
+        res = [sb(f"res{t}", [P, S], F32) for t in range(PACK)]
+        res_bf = sb("res_bf", [P, S, PACK], BF16)
+        out_rows = out_0.rearrange("(p t) j -> p t j", t=PACK)
+        pa = sb("pa", [P, PACK, W], F32)
+        pb = sb("pb", [P, PACK, W], F32)
+        size = sb("size", [P, PACK, W], F32)
+        rt = sb("rt", [P, PACK, W], F32)
+        iv = sb("iv", [P, PACK, W], F32)
+        big = sb("big", [P, PACK, W], F32)
+
+        def fetch(t):
+            nc.vector.tensor_copy(pb[:, t, :], h[t][:].indirect(n4_l[:]))
+            nc.vector.tensor_copy(pa[:, t, :], h[t][:].indirect(n3_l[:]))
+            nc.scalar.activation(size[:, t, :], pb[:, t, :], ACT.Abs)
+            nc.scalar.activation(rt[:, t, :], size[:, t, :], ACT.Abs_reciprocal_sqrt, bias=half[:])
+            nc.scalar.activation(iv[:, t, :], rt[:, t, :], ACT.Square)
+
+        def larger(t):
+            nc.vector.tensor_tensor(big[:, t, :], pa[:, t, :], pb[:, t, :], ALU.max)
+
+        def put_larger(t):
+            nc.vector.tensor_copy(res[t][:].indirect(n4_l[:]), big[:, t, :])
+
+        def put_ratio(t):
+            nc.vector.tensor_tensor(res[t][:].indirect(n3_l[:]), pa[:, t, :], iv[:, t, :], ALU.mult)
+            nc.sync.dma_start(out_rows[:, t, :], res[t][:])
+            rounded = slice(0, S) if t < 2 else halves[1]
+            nc.scalar.copy(res_bf[:, rounded, t], res[t][:, rounded])
+
+        for step in range(PACK + 3):
+            for stage, lag in ((fetch, 0), (larger, 1), (put_larger, 2), (put_ratio, 3)):
+                if 0 <= step - lag < PACK:
+                    stage(step - lag)
+        for t in range(2, PACK):
+            nc.vector.tensor_copy(res_bf[:, halves[0], t], res[t][:, halves[0]])
+
+        o_wd = sb("o_wd", [P, S], U32)
+        o_sc = sb("o_sc", [P, S], U8)
+        out_words = out_1[0].rearrange("p n r -> p (n r)").bitcast(I32)
+        for cols in halves:
+            nc.vector.quantize_mx(o_wd[:, cols].bitcast(FP8X4), o_sc[:, cols], res_bf[:, cols, :].rearrange("p c t -> p (c t)"))
+            nc.sync.dma_start(out_words[:, cols], o_wd[:, cols].bitcast(I32))
+        for q in range(4):
+            queue = nc.scalar if q < 3 else nc.sync
+            queue.dma_start(out_2[0, 4 * q : 4 * q + 4, :].bitcast(I32), o_sc[32 * q : 32 * q + 4, :].bitcast(I32))

@@ -29,8 +29,8 @@ def tile_picked_twqnormbratio_none_po_kernel(
         keep = ctx.enter_context(tc.tile_pool(name="keep", bufs=1))
         psum = ctx.enter_context(tc.psum_pool(name="psum", bufs=1))
 
-        def sb(name, shape, dtype):
-            return keep.tile(shape, dtype, name=name, align_bytes=64)
+        def sb(name, shape, dtype, tag=None):
+            return keep.tile(shape, dtype, name=name, tag=tag or name, align_bytes=64)
 
         def load_list(name, src):
             t = keep.tile(list(src.shape), U16, name=name)
@@ -42,9 +42,9 @@ def tile_picked_twqnormbratio_none_po_kernel(
             nc.sync.dma_start(t[:].bitcast(I32), src[0].rearrange("p n r -> p (n r)").bitcast(I32))
             return t
 
-        def load_scale_rows(queue, t, first, src):
+        def load_scale_rows(queues, t, first, src):
             for q in range(4):
-                queue.dma_start(
+                queues[q].dma_start(
                     t[32 * q + first : 32 * q + first + 4, :].bitcast(I32),
                     src[0, 4 * q : 4 * q + 4, :].bitcast(I32),
                 )
@@ -58,18 +58,20 @@ def tile_picked_twqnormbratio_none_po_kernel(
         dk_plane = sb("dk_plane", [P, H], U8)
         half = sb("half", [P, 1], F32)
         warm = sb("warm", [P, 1], F32)
-        for t in (x_sc, w_sc, d_sc, dk_plane):
+        nc.vector.memset(x_sc[:, : T // 2].bitcast(I32), 0)
+        nc.gpsimd.memset(x_sc[:, T // 2 :].bitcast(I32), 0)
+        for t in (w_sc, d_sc, dk_plane):
             nc.vector.memset(t[:].bitcast(I32), 0)
         nc.vector.memset(half[:], 0.5)
 
-        x_wd = load_words("x_wd", x_words)
         two_l = load_list("two_l", two)
-        load_scale_rows(nc.scalar, x_sc, 0, x_scales)
-        w2_wd = load_words("w2_wd", w2_words)
-        load_scale_rows(nc.scalar, w_sc, 0, w2_scales)
-        load_scale_rows(nc.sync, w_sc, 4, w1_scales)
-        nc.scalar.activation(warm[:], half[:], ACT.Abs_reciprocal_sqrt)
         offs_l = load_list("offs_l", offs)
+        load_scale_rows([nc.scalar, nc.scalar, nc.sync, nc.sync], x_sc, 0, x_scales)
+        x_wd = load_words("x_wd", x_words)
+        w2_wd = load_words("w2_wd", w2_words)
+        load_scale_rows([nc.scalar] * 4, w_sc, 0, w2_scales)
+        load_scale_rows([nc.scalar, nc.scalar, nc.sync, nc.sync], w_sc, 4, w1_scales)
+        nc.scalar.activation(warm[:], half[:], ACT.Abs_reciprocal_sqrt)
         w1_wd = load_words("w1_wd", w1_words)
         nc.sync.dma_start(d_sc[0:P:8, :].bitcast(I32), d_scales[0].bitcast(I32))
         k1_l = load_list("k1_l", k1)
@@ -84,23 +86,24 @@ def tile_picked_twqnormbratio_none_po_kernel(
         neg_gain = sb("neg_gain", [P, PACK], F32)
         nc.scalar.activation(neg_gain[:], gain[:], ACT.Copy, scale=-1.0)
 
-        def pick(name, table, lst, dtype):
-            t = sb(name, [P, S], dtype)
+        def pick(name, table, lst, dtype, tag=None):
+            t = sb(name, [P, S], dtype, tag)
             nc.vector.tensor_copy(t[:], table[:].indirect(lst[:]))
             return t
 
-        x2_wd = pick("x2_wd", x_wd, two_l, U32)
         x2_sc = pick("x2_sc", x_sc, two_l, U8)
+        x1_sc = pick("x1_sc", x_sc, offs_l, U8)
+        x2_wd = pick("x2_wd", x_wd, two_l, U32)
         w2_dealt = sb("w2_dealt", [P, H], I32)
         deal(w2_dealt, w2_wd[:].bitcast(I32))
         w_sc_dealt = sb("w_sc_dealt", [P, H], U8)
         deal(w_sc_dealt, w_sc)
-        x1_wd = pick("x1_wd", x_wd, offs_l, U32)
-        x1_sc = pick("x1_sc", x_sc, offs_l, U8)
+        x1_wd = pick("x1_wd", x_wd, offs_l, U32, "w_sc")
         w1_dealt = sb("w1_dealt", [P, H], I32)
         deal(w1_dealt, w1_wd[:].bitcast(I32))
 
         dk_sc = pick("dk_sc", d_sc, k1_l, U8)
+        dk_wd = pick("dk_wd", d_wd, k1_l, U32)
         dk_sc_dealt = sb("dk_sc_dealt", [P, H], U8)
         deal(dk_sc_dealt, dk_sc)
         for q in range(4):
@@ -108,7 +111,6 @@ def tile_picked_twqnormbratio_none_po_kernel(
                 dk_plane[32 * q : 32 * q + 4, :].bitcast(I32),
                 dk_sc_dealt[32 * q : 32 * q + 32 : 8, :].bitcast(I32),
             )
-        dk_wd = pick("dk_wd", d_wd, k1_l, U32)
         dk_dealt = sb("dk_dealt", [P, H], I32)
         deal(dk_dealt, dk_wd[:].bitcast(I32))
 
@@ -186,46 +188,54 @@ def tile_picked_twqnormbratio_none_po_kernel(
             ratio(cols)
         for cols in quarters:
             quantize_z(cols)
-        h_hi = [psum.tile([P, S], F32, name=f"h_hi{t}", tag=f"bank{4 + t}") for t in range(PACK)]
-        for cols in quarters:
-            for t in range(PACK):
-                coded(h_hi[t], t, cols)
-        for t in range(PACK):
-            nc.scalar.activation(h[t][:, halves[1]], h_hi[t][:, halves[1]], ACT.Copy, scale=0.0625)
+        for pair in range(0, PACK, 2):
+            for u, cols in enumerate(quarters):
+                for t in (pair, pair + 1):
+                    acc = psum.tile([P, S], F32, name=f"h_hi{t}_{u}", tag=f"bank{(4 + 4 * u) % 8 + t}")
+                    coded(acc, t, cols)
+                    nc.scalar.activation(h[t][:, cols], acc[:, cols], ACT.Copy, scale=0.0625)
 
         res = [sb(f"res{t}", [P, S], F32) for t in range(PACK)]
         res_bf = sb("res_bf", [P, S, PACK], BF16)
         out_rows = out_0.rearrange("(p t) j -> p t j", t=PACK)
         pa = sb("pa", [P, PACK, W], F32)
-        pb = sb("pb", [P, PACK, W], F32)
-        size = sb("size", [P, PACK, W], F32)
-        rt = sb("rt", [P, PACK, W], F32)
+        gap = sb("gap", [P, PACK, W], F32)
+        rise = sb("rise", [P, PACK, W], F32)
         iv = sb("iv", [P, PACK, W], F32)
-        big = sb("big", [P, PACK, W], F32)
+        h_abs = sb("h_abs", [P, PACK, S], F32)
+        h_log = [sb(f"h_log{t}", [P, S], F32) for t in range(PACK)]
 
         def fetch(t):
-            nc.vector.tensor_copy(pb[:, t, :], h[t][:].indirect(n4_l[:]))
             nc.vector.tensor_copy(pa[:, t, :], h[t][:].indirect(n3_l[:]))
-            nc.scalar.activation(size[:, t, :], pb[:, t, :], ACT.Abs)
-            nc.scalar.activation(rt[:, t, :], size[:, t, :], ACT.Abs_reciprocal_sqrt, bias=half[:])
-            nc.scalar.activation(iv[:, t, :], rt[:, t, :], ACT.Square)
 
-        def larger(t):
-            nc.vector.tensor_tensor(big[:, t, :], pa[:, t, :], pb[:, t, :], ALU.max)
+        def difference(t):
+            nc.vector.tensor_tensor(gap[:, t, :], h[t][:].indirect(n4_l[:]), pa[:, t, :], ALU.subtract)
 
-        def put_larger(t):
-            nc.vector.tensor_copy(res[t][:].indirect(n4_l[:]), big[:, t, :])
+        def logarithm(t):
+            nc.scalar.activation(h_log[t][:], h_abs[:, t, :], ACT.Ln, bias=half[:])
 
-        def put_ratio(t):
+        def excess(t):
+            nc.scalar.activation(rise[:, t, :], gap[:, t, :], ACT.Relu)
+
+        for t in range(PACK):
+            nc.scalar.activation(h_abs[:, t, :], h[t][:], ACT.Abs)
+        for pair in range(0, PACK, 2):
+            for stage in (fetch, difference):
+                for t in (pair, pair + 1):
+                    stage(t)
+        for step in range(PACK + 2):
+            for stage, lag in ((logarithm, 2), (excess, 0)):
+                if 0 <= step - lag < PACK:
+                    stage(step - lag)
+        for t in range(PACK):
+            nc.vector.tensor_tensor(res[t][:].indirect(n4_l[:]), pa[:, t, :], rise[:, t, :], ALU.add)
+        for t in range(PACK):
+            nc.scalar.activation(iv[:, t, :], h_log[t][:].indirect(n4_l[:]), ACT.Exp, scale=-1.0)
+        for t in range(PACK):
             nc.vector.tensor_tensor(res[t][:].indirect(n3_l[:]), pa[:, t, :], iv[:, t, :], ALU.mult)
             nc.sync.dma_start(out_rows[:, t, :], res[t][:])
             rounded = slice(0, S) if t < 2 else halves[1]
             nc.scalar.copy(res_bf[:, rounded, t], res[t][:, rounded])
-
-        for step in range(PACK + 3):
-            for stage, lag in ((fetch, 0), (larger, 1), (put_larger, 2), (put_ratio, 3)):
-                if 0 <= step - lag < PACK:
-                    stage(step - lag)
         for t in range(2, PACK):
             nc.vector.tensor_copy(res_bf[:, halves[0], t], res[t][:, halves[0]])
 

from contextlib import ExitStack

import concourse.mybir as mybir

K, T, S, H, G, W = 512, 1024, 512, 512, 2048, 256
FLOPS = 3 * 2 * K * H * S

F32 = mybir.dt.float32
BF16 = mybir.dt.bfloat16
I32 = mybir.dt.int32
U32 = mybir.dt.uint32
U16 = mybir.dt.uint16
U8 = mybir.dt.uint8
FP8X4 = mybir.dt.float8_e4m3fn_x4
ACT = mybir.ActivationFunctionType
ALU = mybir.AluOpType

P = 128
PACK = 4
HALF = S // 2


def tile_picked_twqnormbratio_none_po_kernel(
    tc, x_words, x_scales, w1_words, w1_scales, w2_words, w2_scales, gs, d_words, d_scales,
    offs, two, n1, n2, k1, n3, n4, out_0, out_1, out_2,
):
    nc = tc.nc
    with ExitStack() as ctx:
        keep = ctx.enter_context(tc.tile_pool(name="keep", bufs=1))
        psum = ctx.enter_context(tc.psum_pool(name="psum", bufs=1))

        def sb(name, shape, dtype, tag=None):
            return keep.tile(shape, dtype, name=name, tag=tag or name, align_bytes=64)

        def load_list(name, src):
            t = keep.tile(list(src.shape), U16, name=name)
            nc.sync.dma_start(t[:], src)
            return t

        def load_words(name, src):
            t = sb(name, [P, src.shape[2]], U32)
            nc.sync.dma_start(t[:].bitcast(I32), src[0].rearrange("p n r -> p (n r)").bitcast(I32))
            return t

        def load_scale_rows(queues, t, first, src):
            for q in range(4):
                queues[q].dma_start(
                    t[32 * q + first : 32 * q + first + 4, :].bitcast(I32),
                    src[0, 4 * q : 4 * q + 4, :].bitcast(I32),
                )

        def deal(dst, src):
            nc.vector.tensor_copy(dst[:].rearrange("p (t m) -> p m t", t=PACK), src[:].rearrange("p (m t) -> p m t", t=PACK))

        x_sc = sb("x_sc", [P, T], U8)
        w_sc = sb("w_sc", [P, H], U8)
        d_sc = sb("d_sc", [P, G], U8)
        dk_plane = sb("dk_plane", [P, H], U8)
        half = sb("half", [P, 1], F32)
        warm = sb("warm", [P, 1], F32)
        nc.vector.memset(x_sc[:, : T // 2].bitcast(I32), 0)
        nc.gpsimd.memset(x_sc[:, T // 2 :].bitcast(I32), 0)
        for t in (w_sc, d_sc, dk_plane):
            nc.vector.memset(t[:].bitcast(I32), 0)
        nc.vector.memset(half[:], 0.5)

        two_l = load_list("two_l", two)
        offs_l = load_list("offs_l", offs)
        load_scale_rows([nc.scalar, nc.scalar, nc.sync, nc.sync], x_sc, 0, x_scales)
        x_wd = load_words("x_wd", x_words)
        w2_wd = load_words("w2_wd", w2_words)
        load_scale_rows([nc.scalar] * 4, w_sc, 0, w2_scales)
        load_scale_rows([nc.scalar, nc.scalar, nc.sync, nc.sync], w_sc, 4, w1_scales)
        nc.scalar.activation(warm[:], half[:], ACT.Abs_reciprocal_sqrt)
        w1_wd = load_words("w1_wd", w1_words)
        nc.sync.dma_start(d_sc[0:P:8, :].bitcast(I32), d_scales[0].bitcast(I32))
        k1_l = load_list("k1_l", k1)
        d_wd = load_words("d_wd", d_words)
        n2_l = load_list("n2_l", n2)
        gain = sb("gain", [P, PACK], F32)
        nc.sync.dma_start(gain[:], gs.rearrange("(p t) o -> p (t o)", t=PACK))
        n1_l = load_list("n1_l", n1)
        n3_l = load_list("n3_l", n3)
        n4_l = load_list("n4_l", n4)

        neg_gain = sb("neg_gain", [P, PACK], F32)
        nc.scalar.activation(neg_gain[:], gain[:], ACT.Copy, scale=-1.0)

        def pick(name, table, lst, dtype, tag=None):
            t = sb(name, [P, S], dtype, tag)
            nc.vector.tensor_copy(t[:], table[:].indirect(lst[:]))
            return t

        x2_sc = pick("x2_sc", x_sc, two_l, U8)
        x1_sc = pick("x1_sc", x_sc, offs_l, U8)
        x2_wd = pick("x2_wd", x_wd, two_l, U32)
        w2_dealt = sb("w2_dealt", [P, H], I32)
        deal(w2_dealt, w2_wd[:].bitcast(I32))
        w_sc_dealt = sb("w_sc_dealt", [P, H], U8)
        deal(w_sc_dealt, w_sc)
        x1_wd = pick("x1_wd", x_wd, offs_l, U32, "w_sc")
        w1_dealt = sb("w1_dealt", [P, H], I32)
        deal(w1_dealt, w1_wd[:].bitcast(I32))

        dk_sc = pick("dk_sc", d_sc, k1_l, U8)
        dk_wd = pick("dk_wd", d_wd, k1_l, U32)
        dk_sc_dealt = sb("dk_sc_dealt", [P, H], U8)
        deal(dk_sc_dealt, dk_sc)
        for q in range(4):
            nc.sync.dma_start(
                dk_plane[32 * q : 32 * q + 4, :].bitcast(I32),
                dk_sc_dealt[32 * q : 32 * q + 32 : 8, :].bitcast(I32),
            )
        dk_dealt = sb("dk_dealt", [P, H], I32)
        deal(dk_dealt, dk_wd[:].bitcast(I32))

        def rows(t):
            return slice(P * t, P * (t + 1))

        d_abs, d_abs2, y_win, y_plain = [], [], [], []
        for t in range(PACK):
            acc = psum.tile([P, S], F32, name=f"d_acc{t}", tag=f"bank{t}")
            nc.tensor.matmul_mx(acc[:], lhsT=w2_dealt[:, rows(t)].bitcast(FP8X4), lhsT_scale=w_sc_dealt[:, rows(t)],
                                rhs=x2_wd[:].bitcast(FP8X4), rhs_scale=x2_sc[:], start=True, stop=True)
            d_abs.append(sb(f"d_abs{t}", [P, S], F32))
            d_abs2.append(sb(f"d_own{t}", [P, S], F32))
            nc.scalar.activation(d_abs[t][:], acc[:], ACT.Abs)
            nc.scalar.activation(d_abs2[t][:], acc[:], ACT.Abs)
        for t in range(PACK):
            acc = psum.tile([P, S], F32, name=f"y_acc{t}", tag=f"bank{4 + t}")
            nc.tensor.matmul_mx(acc[:], lhsT=w1_dealt[:, rows(t)].bitcast(FP8X4), lhsT_scale=w_sc_dealt[4:P, rows(t)],
                                rhs=x1_wd[:].bitcast(FP8X4), rhs_scale=x1_sc[:], start=True, stop=True)
            y_win.append(sb(f"y_win{t}", [P, S], F32))
            y_plain.append(sb(f"y_own{t}", [P, S], F32))
            nc.scalar.activation(y_win[t][:], acc[:], ACT.Copy, scale=neg_gain[:, t : t + 1])
            nc.scalar.activation(y_plain[t][:], acc[:], ACT.Copy, scale=neg_gain[:, t : t + 1])

        den = sb("den", [P, PACK, S], F32)
        root = sb("root", [P, PACK, S], F32)
        inv = sb("inv", [P, PACK, S], F32)
        num = sb("num", [P, PACK, S], F32)
        z = sb("z", [P, S, PACK], BF16)
        z_wd = sb("z_wd", [P, S], U32)
        z_sc = sb("z_sc", [P, S], U8)
        h = [sb(f"h{t}", [P, S], F32) for t in range(PACK)]

        halves = [slice(HALF * u, HALF * (u + 1)) for u in range(2)]
        quarters = [slice(HALF, HALF + HALF // 2), slice(HALF + HALF // 2, S)]

        def entries(cols):
            return slice(cols.start // 16, cols.stop // 16)

        def numerator(t, cols):
            nc.vector.tensor_tensor(num[:, t, cols], y_win[t][:].indirect(n1_l[:, entries(cols)]), y_plain[t][:, cols], ALU.subtract)

        def ratio(cols):
            nc.vector.tensor_tensor(
                z[:, cols, :].rearrange("p (c i) t -> p c t i", i=4),
                num[:, :, cols].rearrange("p t (c i) -> p c t i", i=4),
                inv[:, :, cols].rearrange("p t (c i) -> p c t i", i=4),
                ALU.mult,
            )

        def quantize_z(cols):
            nc.vector.quantize_mx(z_wd[:, cols].bitcast(FP8X4), z_sc[:, cols], z[:, cols, :].rearrange("p c t -> p (c t)"))

        def coded(acc, t, cols):
            nc.tensor.matmul_mx(acc[:, cols], lhsT=dk_dealt[:, rows(t)].bitcast(FP8X4), lhsT_scale=dk_plane[:, rows(t)],
                                rhs=z_wd[:, cols].bitcast(FP8X4), rhs_scale=z_sc[:, cols], start=True, stop=True)

        for cols in halves:
            for t in range(PACK):
                nc.vector.tensor_tensor(den[:, t, cols], d_abs[t][:].indirect(n2_l[:, entries(cols)]), d_abs2[t][:, cols], ALU.add)
                nc.scalar.activation(root[:, t, cols], den[:, t, cols], ACT.Abs_reciprocal_sqrt, bias=half[:])
                nc.scalar.activation(inv[:, t, cols], root[:, t, cols], ACT.Square)
        for t in range(PACK):
            numerator(t, halves[0])
        for t in range(PACK - 1):
            numerator(t, halves[1])
        ratio(halves[0])
        numerator(PACK - 1, halves[1])
        quantize_z(halves[0])
        for t in range(PACK):
            acc = psum.tile([P, S], F32, name=f"h_lo{t}", tag=f"bank{t}")
            coded(acc, t, halves[0])
            nc.scalar.activation(h[t][:, halves[0]], acc[:, halves[0]], ACT.Copy, scale=0.0625)
        for cols in quarters:
            ratio(cols)
        for cols in quarters:
            quantize_z(cols)
        for pair in range(0, PACK, 2):
            for u, cols in enumerate(quarters):
                for t in (pair, pair + 1):
                    acc = psum.tile([P, S], F32, name=f"h_hi{t}_{u}", tag=f"bank{(4 + 4 * u) % 8 + t}")
                    coded(acc, t, cols)
                    nc.scalar.activation(h[t][:, cols], acc[:, cols], ACT.Copy, scale=0.0625)

        res = [sb(f"res{t}", [P, S], F32) for t in range(PACK)]
        res_bf = sb("res_bf", [P, S, PACK], BF16)
        out_rows = out_0.rearrange("(p t) j -> p t j", t=PACK)
        pa = sb("pa", [P, PACK, W], F32)
        gap = sb("gap", [P, PACK, W], F32)
        rise = sb("rise", [P, PACK, W], F32)
        iv = sb("iv", [P, PACK, W], F32)
        h_abs = sb("h_abs", [P, PACK, S], F32)
        h_log = [sb(f"h_log{t}", [P, S], F32) for t in range(PACK)]

        def fetch(t):
            nc.vector.tensor_copy(pa[:, t, :], h[t][:].indirect(n3_l[:]))

        def difference(t):
            nc.vector.tensor_tensor(gap[:, t, :], h[t][:].indirect(n4_l[:]), pa[:, t, :], ALU.subtract)

        def logarithm(t):
            nc.scalar.activation(h_log[t][:], h_abs[:, t, :], ACT.Ln, bias=half[:])

        def excess(t):
            nc.scalar.activation(rise[:, t, :], gap[:, t, :], ACT.Relu)

        for t in range(PACK):
            nc.scalar.activation(h_abs[:, t, :], h[t][:], ACT.Abs)
        for pair in range(0, PACK, 2):
            for stage in (fetch, difference):
                for t in (pair, pair + 1):
                    stage(t)
        for step in range(PACK + 2):
            for stage, lag in ((logarithm, 2), (excess, 0)):
                if 0 <= step - lag < PACK:
                    stage(step - lag)
        for t in range(PACK):
            nc.vector.tensor_tensor(res[t][:].indirect(n4_l[:]), pa[:, t, :], rise[:, t, :], ALU.add)
        for t in range(PACK):
            nc.scalar.activation(iv[:, t, :], h_log[t][:].indirect(n4_l[:]), ACT.Exp, scale=-1.0)
        for t in range(PACK):
            nc.vector.tensor_tensor(res[t][:].indirect(n3_l[:]), pa[:, t, :], iv[:, t, :], ALU.mult)
            nc.sync.dma_start(out_rows[:, t, :], res[t][:])
            rounded = slice(0, S) if t < 2 else halves[1]
            nc.scalar.copy(res_bf[:, rounded, t], res[t][:, rounded])
        for t in range(2, PACK):
            nc.vector.tensor_copy(res_bf[:, halves[0], t], res[t][:, halves[0]])

        o_wd = sb("o_wd", [P, S], U32)
        o_sc = sb("o_sc", [P, S], U8)
        out_words = out_1[0].rearrange("p n r -> p (n r)").bitcast(I32)
        for cols in halves:
            nc.vector.quantize_mx(o_wd[:, cols].bitcast(FP8X4), o_sc[:, cols], res_bf[:, cols, :].rearrange("p c t -> p (c t)"))
            nc.sync.dma_start(out_words[:, cols], o_wd[:, cols].bitcast(I32))
        for q in range(4):
            queue = nc.scalar if q < 3 else nc.sync
            queue.dma_start(out_2[0, 4 * q : 4 * q + 4, :].bitcast(I32), o_sc[32 * q : 32 * q + 4, :].bitcast(I32))
